import numpy as np
CORES = [1,129,9,137,17,145,25,153,33,161,41,169,49,177,57,185,65,193,73,201,81,209,89,217,97,225,105,233,113,241,121,249]
N = 32
GROUPS = [[0,1],[2,3],[4,5],[6,7],[8,9],[10,11],[12,13],[14,15],[16,17],[18,19],[20,21],[22,23],[24,25],[26,27],[28,29],[30,31]]
def setup_inputs(rng):
    return {"x": rng.standard_normal((N, 128, 1024), dtype=np.float32)}
def reference(x):
    y = np.empty((N, 128, 1024), x.dtype)
    for g in GROUPS:
        s = x[g].sum(axis=0, dtype=np.float64).astype(x[g].dtype)
        for r in g:
            y[r] = s
    return {"y": y}

@@ -1,0 +1,28 @@
+from concourse.mybir import AluOpType
+
+SCRATCH = {
+    "xs": ("sbuf", [128, 1024], "float32"),
+    "land": ("sbuf", [128, 1024], "float32"),
+}
+SEMAPHORES = ["loaded", "copied", "sent", "arrived", "stored"]
+
+
+def rank_program(g, core, T, topo):
+    rank = T.rank_of(core)
+    if rank is None:
+        return
+    peer = None
+    for grp in T.tables["GROUPS"]:
+        if rank in grp:
+            peer = T.cores[[r for r in grp if r != rank][0]]
+    rid, pid = topo.addr(peer, core)
+
+    g.sync.dma_start(T.xs[:], T.x[:]).then_inc(T.sem.loaded, 16)
+    g.scalar.dma_start(T.y[:], T.x[:]).then_inc(T.sem.copied, 16)
+    g.wait_ge(T.sem.loaded, 16)
+    g.remote_dma(T.land[:], T.xs[:], T.sem.arrived, T.sem.sent, pid, rid, 0x00FF)
+    g.wait_ge(T.sem.arrived, 8)
+    g.wait_ge(T.sem.copied, 16)
+    g.dma_start(T.y[:], T.land[:], accum_op=AluOpType.add).then_inc(T.sem.stored, 16)
+    g.wait_ge(T.sem.stored, 16)
+    g.wait_ge(T.sem.sent, 8)

@@ -1,28 +1,57 @@
 from concourse.mybir import AluOpType
 
+W = 1024
+H = W // 2
 SCRATCH = {
-    "xs": ("sbuf", [128, 1024], "float32"),
-    "land": ("sbuf", [128, 1024], "float32"),
+    "xs": ("sbuf", [128, W], "float32"),
+    "land": ("sbuf", [128, W], "float32"),
 }
-SEMAPHORES = ["loaded", "copied", "sent", "arrived", "stored"]
+SEMAPHORES = ["load_d", "load_r", "copied", "sent", "relay", "arr_d", "arr_r", "stored"]
+ON_CHIP, OFF_CHIP = 0xFFFF, 0x00FF
+HELPER = 4
+
+
+def partner_of(rank, T):
+    for grp in T.tables["GROUPS"]:
+        if rank in grp:
+            return T.cores[[r for r in grp if r != rank][0]]
+    return None
 
 
 def rank_program(g, core, T, topo):
+    s = T.sem
     rank = T.rank_of(core)
-    if rank is None:
-        return
-    peer = None
-    for grp in T.tables["GROUPS"]:
-        if rank in grp:
-            peer = T.cores[[r for r in grp if r != rank][0]]
-    rid, pid = topo.addr(peer, core)
 
-    g.sync.dma_start(T.xs[:], T.x[:]).then_inc(T.sem.loaded, 16)
-    g.scalar.dma_start(T.y[:], T.x[:]).then_inc(T.sem.copied, 16)
-    g.wait_ge(T.sem.loaded, 16)
-    g.remote_dma(T.land[:], T.xs[:], T.sem.arrived, T.sem.sent, pid, rid, 0x00FF)
-    g.wait_ge(T.sem.arrived, 8)
-    g.wait_ge(T.sem.copied, 16)
-    g.dma_start(T.y[:], T.land[:], accum_op=AluOpType.add).then_inc(T.sem.stored, 16)
-    g.wait_ge(T.sem.stored, 16)
-    g.wait_ge(T.sem.sent, 8)
+    if rank is None:
+        owner = core - HELPER
+        if owner < 0 or T.rank_of(owner) is None:
+            return
+        peer = partner_of(T.rank_of(owner), T)
+        rid, pid = topo.addr(peer, core)
+        g.wait_ge(s.relay, 16)
+        g.remote_dma(T.land[:, H:W], T.land[:, H:W], s.arr_r, s.sent, pid, rid, OFF_CHIP)
+        g.wait_ge(s.sent, 8)
+        return
+
+    peer = partner_of(rank, T)
+    helper = core + HELPER
+    assert topo.chip(helper) == topo.chip(core) and topo.die(helper) != topo.die(core)
+
+    g.sync.dma_start(T.xs[:, H:W], T.x[:, H:W]).then_inc(s.load_r, 16)
+    g.scalar.dma_start(T.xs[:, 0:H], T.x[:, 0:H]).then_inc(s.load_d, 16)
+    g.scalar.dma_start(T.y[:], T.x[:]).then_inc(s.copied, 16)
+
+    rid, pid = topo.addr(helper, core)
+    g.wait_ge(s.load_r, 16)
+    g.remote_dma(T.land[:, H:W], T.xs[:, H:W], s.relay, s.sent, pid, rid, ON_CHIP)
+    rid, pid = topo.addr(peer, core)
+    g.wait_ge(s.load_d, 16)
+    g.remote_dma(T.land[:, 0:H], T.xs[:, 0:H], s.arr_d, s.sent, pid, rid, OFF_CHIP)
+
+    g.wait_ge(s.copied, 16)
+    g.wait_ge(s.arr_d, 8)
+    g.dma_start(T.y[:, 0:H], T.land[:, 0:H], accum_op=AluOpType.add).then_inc(s.stored, 16)
+    g.wait_ge(s.arr_r, 8)
+    g.dma_start(T.y[:, H:W], T.land[:, H:W], accum_op=AluOpType.add).then_inc(s.stored, 16)
+    g.wait_ge(s.stored, 32)
+    g.wait_ge(s.sent, 16 + 8)

from concourse.mybir import AluOpType

W = 1024
H = W // 2
SCRATCH = {
    "xs": ("sbuf", [128, W], "float32"),
    "land": ("sbuf", [128, W], "float32"),
}
SEMAPHORES = ["load_d", "load_r", "copied", "sent", "relay", "arr_d", "arr_r", "stored"]
ON_CHIP, OFF_CHIP = 0xFFFF, 0x00FF
HELPER = 4


def partner_of(rank, T):
    for grp in T.tables["GROUPS"]:
        if rank in grp:
            return T.cores[[r for r in grp if r != rank][0]]
    return None


def rank_program(g, core, T, topo):
    s = T.sem
    rank = T.rank_of(core)

    if rank is None:
        owner = core - HELPER
        if owner < 0 or T.rank_of(owner) is None:
            return
        peer = partner_of(T.rank_of(owner), T)
        rid, pid = topo.addr(peer, core)
        g.wait_ge(s.relay, 16)
        g.remote_dma(T.land[:, H:W], T.land[:, H:W], s.arr_r, s.sent, pid, rid, OFF_CHIP)
        g.wait_ge(s.sent, 8)
        return

    peer = partner_of(rank, T)
    helper = core + HELPER
    assert topo.chip(helper) == topo.chip(core) and topo.die(helper) != topo.die(core)

    g.sync.dma_start(T.xs[:, H:W], T.x[:, H:W]).then_inc(s.load_r, 16)
    g.scalar.dma_start(T.xs[:, 0:H], T.x[:, 0:H]).then_inc(s.load_d, 16)
    g.scalar.dma_start(T.y[:], T.x[:]).then_inc(s.copied, 16)

    rid, pid = topo.addr(helper, core)
    g.wait_ge(s.load_r, 16)
    g.remote_dma(T.land[:, H:W], T.xs[:, H:W], s.relay, s.sent, pid, rid, ON_CHIP)
    rid, pid = topo.addr(peer, core)
    g.wait_ge(s.load_d, 16)
    g.remote_dma(T.land[:, 0:H], T.xs[:, 0:H], s.arr_d, s.sent, pid, rid, OFF_CHIP)

    g.wait_ge(s.copied, 16)
    g.wait_ge(s.arr_d, 8)
    g.dma_start(T.y[:, 0:H], T.land[:, 0:H], accum_op=AluOpType.add).then_inc(s.stored, 16)
    g.wait_ge(s.arr_r, 8)
    g.dma_start(T.y[:, H:W], T.land[:, H:W], accum_op=AluOpType.add).then_inc(s.stored, 16)
    g.wait_ge(s.stored, 32)
    g.wait_ge(s.sent, 16 + 8)
